import numpy as np, ml_dtypes
CORES = [52,68,84,180,196,212,308,324,340]
N = 9
import mx_ref
NC, G = 128, 2
C = np.float32(0.047)
BF = ml_dtypes.bfloat16
def cut(t, i, w=512):
    return t[:, w * i:w * i + w]
def tile(rs):
    return np.stack(rs, axis=2).reshape(128, -1).astype(BF)
def layer(w, X):
    out = []
    for i in range(G):
        for t in range(len(X)):
            p = mx_ref.matmul(mx_ref.quantize(cut(w, len(X) * i + t)), X[t])
            z = p if t == 0 else z + p
        out.append(z)
    return out
def act(Z):
    return [np.maximum(s * z, 0) * C for z in Z for s in (1, -1)]
def setup_inputs(rng):
    def f(*shape):
        return mx_ref.flush((rng.standard_normal(shape, dtype=np.float32) * np.exp2(rng.integers(-2, 3, shape[:-1] + (1,)))).astype(BF))
    return {"x": f(N, 128, 4 * NC), "w1": f(N, 128, G * 512), "w2": f(N, 128, 512)}
def setup_inputs_blocks(rng):
    d = setup_inputs(rng)
    for k in ("x", "w1", "w2"): d[k] = mx_ref.spread(d[k], rng, 2)
    return d
def setup_inputs_wide(rng):
    d = setup_inputs(rng)
    for k in ("x", "w1", "w2"): d[k] = mx_ref.flush((d[k].astype(np.float32) * np.exp2(rng.integers(-6, 7, (N, 1, 1))).astype(np.float32)).astype(BF))
    return d
def reference(x, w1, w2):
    X = [mx_ref.quantize(x[j]) for j in range(N)]
    y = np.zeros((N, 128, NC), np.float32)
    for c in range(N):
        for r in range(N):
            p = mx_ref.matmul(mx_ref.quantize(w2[r]), mx_ref.quantize(tile(act(layer(w1[r], [X[c]])))))
            y[c] = p if r == 0 else y[c] + p
    return {"y": y}

@@ -1,0 +1,313 @@
+import numpy as np
+from concourse.bass import DstId, RemoteDMATransfer
+from concourse.mybir import dt, AluOpType, ActivationFunctionType
+
+C = float(np.float32(0.047))
+X, W = 128, 384
+F8, U8, BF, F32 = "float8_e4m3fn_x4", "uint8", "bfloat16", "float32"
+
+SCRATCH = {
+    "xin": ("sbuf", [128, 512], BF), "w1in": ("sbuf", [128, 1024], BF), "w2in": ("sbuf", [128, 512], BF),
+    "h": ("sbuf", [128, 4 * 1152], BF),
+    "so": ("sbuf", [128, 8 * 128], F32),
+    "si": ("sbuf", [128, 8 * 128], F32),
+    "acc": ("sbuf", [128, 128], F32),
+    "pz": ("psum", [128, 2048], F32),
+    "po": ("psum", [128, 2048], F32),
+}
+for _n, _w in (("s", 640),
+               ("a", 1152),
+               ("t", 512),
+               ("m", 384),
+               ("f0", 768),
+               ("f1", 768),
+               ("h", 1152)):
+    SCRATCH["q" + _n] = ("sbuf", [128, _w], F8)
+    SCRATCH["p" + _n] = ("sbuf", [128, _w], U8)
+
+EVENTS = 80
+SEMAPHORES = (["lx", "lw1", "lw2", "sent", "stored", "am", "ap0", "ap1", "at", "f0p", "f0x", "f1p", "f1x"]
+              + ["s%d" % i for i in range(8)] + ["e%d" % i for i in range(EVENTS)])
+
+
+def rank_program(g, core, T, topo):
+    if T.rank_of(core) is None:
+        return
+
+    hosts = sorted({topo.host(c) for c in T.cores})
+    group = {h: sorted((c for c in T.cores if topo.host(c) == h), key=topo.chip) for h in hosts}
+    mid = [h for h in hosts if all(topo.may_write(a, b) for a in group[h] for b in T.cores if b != a)][0]
+    ends = [h for h in hosts if h != mid]
+    me = topo.host(core)
+    k = group[me].index(core)
+    n1, n2 = (k + 1) % 3, (k + 2) % 3
+    partner = {h: [c for c in group[h] if topo.chip(c) == topo.chip(core)][0] for h in hosts}
+
+    ev_n = [0]
+
+    def event():
+        ev_n[0] += 1
+        return ["e%d" % (ev_n[0] - 1), 0]
+
+    def inc(call, ev, n=1):
+        call.then_inc(T.sem[ev[0]], n)
+        ev[1] += n
+
+    queues = {"g": g, "T": g.tensor, "V": g.vector, "S": g.scalar, "Y": g.sync}
+    waited = {q: {} for q in queues}
+
+    def need(q, *evs):
+        for ev in evs:
+            if ev is not None and waited[q].get(ev[0], 0) < ev[1]:
+                queues[q].wait_ge(T.sem[ev[0]], ev[1])
+                waited[q][ev[0]] = ev[1]
+
+    sent = ["sent", 0]
+
+    def engines(dst):
+        m = topo.mask(core, dst)
+        return [e for e in range(m.bit_length()) if (m >> e) & 1]
+
+    def send(*transfers):
+        out = []
+        for eng, sem, src, dests in transfers:
+            ids = []
+            for d, _ in dests:
+                rid, pid = topo.addr(d, core)
+                ids.append(DstId(rid=rid, pnc=pid))
+            out.append(RemoteDMATransfer(dst_ids=ids, dma_engine_mask=sum(1 << e for e in eng), remote_sem=T.sem[sem],
+                                         srcs=[src], dsts=[v for _, v in dests]))
+            sent[1] += len(eng)
+        g.remote_dma_fused(out, local_sem=T.sem["sent"])
+
+    def codes(name, a, b):
+        return T["q" + name][:, a:b].bitcast(dt.uint8)
+
+    def scales(name, a, b):
+        return T["p" + name][:, a:b]
+
+    def send_mx(*transfers):
+        for view in (codes, scales):
+            send(*[(eng, sem, view("s", a, a + n), [(d, view(buf, b, b + n)) for d, buf, b in dests])
+                   for eng, sem, a, n, dests in transfers])
+
+    def slot(buf, i, n=1):
+        return T[buf][:, 128 * i:128 * (i + n)]
+
+    lx, lw1, lw2 = ["lx", 16], ["lw1", 16], ["lw2", 16]
+    g.sync.dma_start(T.xin[:], T.x[:]).then_inc(T.sem["lx"], 16)
+    g.scalar.dma_start(T.w1in[:], T.w1[:]).then_inc(T.sem["lw1"], 16)
+    g.sync.dma_start(T.w2in[:], T.w2[:]).then_inc(T.sem["lw2"], 16)
+
+    def quantise(src, name, a, b, ev):
+        inc(g.vector.quantize_mx(T["q" + name][:, a:b], T["p" + name][:, a:b], src[:]), ev)
+
+    qx, qx2, qw = event(), event(), event()
+    need("V", lx)
+    quantise(T.xin, "s", 0, X, qx)
+    if me == mid:
+        quantise(T.xin, "m", X, 2 * X, qx2)
+    else:
+        quantise(T.xin, "s", X + W, 2 * X + W, qx2)
+        quantise(T.xin, "a", W + X, W + 2 * X, qx2)
+    need("V", lw1)
+    quantise(T.w1in, "s", X, X + 256, qw)
+    need("V", lw2)
+    quantise(T.w2in, "s", X + 256, X + W, qw)
+
+    if me == mid:
+        allE = engines(partner[ends[0]])
+        racks = {h: topo.same_plane(core, partner[h]) for h in ends}
+        half = {True: allE[0::2], False: allE[1::2]}
+        need("g", qx)
+        send_mx((allE, "am", 0, X, [(group[mid][j], "m", 0 if (j + 1) % 3 == k else 2 * X) for j in (n1, n2)]))
+        need("g", qw)
+        send_mx(*[(half[racks[h]], "at", 0, X + W, [(partner[h], "t", 0)]) for h in ends])
+    else:
+        t = partner[mid]
+        fn = "f%d" % ends.index(me)
+        allE = engines(t)
+        toX = [(group[mid][j], fn, X * ((k - j - 1) % 3)) for j in (n1, n2)]
+        p1, p2 = group[me][n1], group[me][n2]
+        if topo.same_plane(core, t):
+            need("g", qx)
+            send_mx((allE, fn + "x", 0, X, toX))
+            need("g", qw)
+            send_mx((allE, fn + "p", 0, X + W, [(t, fn, 2 * X)]))
+            need("g", qx2)
+            send_mx((allE[0::2], "ap1", 0, X + W, [(p1, "a", W + 2 * X)]),
+                    (allE[1::2], "ap0", X, X + W, [(p2, "a", 0)]))
+        else:
+            cab, sw = allE[1::2], allE[0::2]
+            need("g", qx, qx2, qw)
+            send_mx((cab, fn + "p", 0, X + W, [(t, fn, 2 * X)]),
+                    (sw[0::2], "ap1", 0, X + W, [(p1, "a", W + 2 * X)]),
+                    (sw[1::2], "ap0", X, X + W, [(p2, "a", 0)]))
+            send_mx((cab, fn + "x", 0, X, toX))
+
+    nE = len(allE)
+    am = ["am", 2 * 2 * nE]
+    at = ["at", nE]
+    ap0, ap1 = ["ap0", nE], ["ap1", nE]
+    if me != mid and not topo.same_plane(core, partner[mid]):
+        ap0, ap1 = ["ap0", nE // 2], ["ap1", nE // 2]
+    fp, fx = {}, {}
+    for i, h in enumerate(ends):
+        near = topo.same_plane(partner[h], partner[mid])
+        fp[h] = ["f%dp" % i, 2 * nE if near else nE]
+        fx[h] = ["f%dx" % i, 2 * 2 * nE if near else 2 * nE]
+
+    zset = {0: [], 1: []}
+    bank_read = {}
+
+    off = [0]
+
+    def batch(need_ev, wbuf, w0, xbuf, x0, n, zs):
+        b = dict(arr=need_ev, w=(wbuf, w0), x=(xbuf, x0), n=n, zs=zs, off=off[0], z=[event(), event()],
+                 r=[event(), event()], q=event())
+        off[0] += n
+        return b
+
+    def mm(out, wname, w0, xname, x0, n, ev, start=True, stop=True):
+        inc(g.tensor.matmul_mx(out, T["q" + wname][:, w0:w0 + 128], T["p" + wname][:, w0:w0 + 128],
+                               T["q" + xname][:, x0:x0 + n], T["p" + xname][:, x0:x0 + n], start, stop), ev)
+
+    def Z(b, which=(0, 1)):
+        need("T", *b["arr"])
+        if 0 in which:
+            need("T", *zset[b["zs"]])
+        for i in which:
+            c0 = 512 * (2 * b["zs"] + i)
+            mm(T.pz[:, c0:c0 + b["n"]], b["w"][0], b["w"][1] + 128 * i, b["x"][0], b["x"][1], b["n"], b["z"][i])
+        zset[b["zs"]] = b["r"]
+
+    def tile_view(b, i):
+        return T.h[:, 4 * b["off"] + i:4 * (b["off"] + b["n"]):4]
+
+    def R01(b, which=(0, 1)):
+        c0 = 512 * 2 * b["zs"]
+        need("S", b["z"][0])
+        for i in which:
+            inc(g.scalar.activation(tile_view(b, i), T.pz[:, c0:c0 + b["n"]], ActivationFunctionType.Relu,
+                                    scale=-C if i else C), b["r"][0])
+
+    def R23(b):
+        c0 = 512 * (2 * b["zs"] + 1)
+        need("V", b["z"][1])
+        for i in (0, 1):
+            inc(g.vector.tensor_scalar(tile_view(b, 2 + i), T.pz[:, c0:c0 + b["n"]], -C if i else C, 0.0,
+                                       AluOpType.mult, AluOpType.max), b["r"][1])
+
+    def Q(b):
+        need("V", b["r"][0], b["r"][1])
+        a, e = b["off"], b["off"] + b["n"]
+        inc(g.vector.quantize_mx(T.qh[:, a:e], T.ph[:, a:e], T.h[:, 4 * a:4 * e]), b["q"])
+
+    def O(b, *outs):
+        need("T", b["q"])
+        for bank, i, m, ev, start, stop in outs:
+            if start:
+                need("T", bank_read.get(bank))
+            mm(T.po[:, 512 * bank:512 * bank + 128 * m], b["w"][0], b["w"][1] + 256, "h", b["off"] + 128 * i, 128 * m,
+               ev, start, stop)
+
+    def copy(bank, i, m, ev):
+        c = event()
+        need("S", ev)
+        inc(g.scalar.activation(slot("so", i, m), T.po[:, 512 * bank:512 * bank + 128 * m],
+                                ActivationFunctionType.Copy), c)
+        bank_read[bank] = c
+        return c
+
+    yo = event()
+    ev = [event() for _ in range(6)]
+    A0, A1 = allE[:nE // 2], allE[nE // 2:]
+    if me == mid:
+        e0, e1 = ends
+        far, near = (e0, e1) if topo.same_plane(core, partner[e1]) else (e1, e0)
+        ff, fnr = "f%d" % ends.index(far), "f%d" % ends.index(near)
+        peer = [group[mid][n1], group[mid][n2]]
+        T1 = batch([qx2, qw, am], "s", X, "m", 0, 384, 0)
+        T2b = batch([fp[far], fp[near]], fnr, 3 * X, ff, 2 * X, 128, 1)
+        T3 = batch([fp[far], fx[near]], ff, 3 * X, fnr, 0, 384, 0)
+        T2a = batch([fx[far]], fnr, 3 * X, ff, 0, 256, 1)
+        Z(T1)
+        R01(T1), R23(T1), Q(T1)
+        O(T1, (1, 0, 1, ev[0], True, True), (2, 2, 1, ev[1], True, True), (0, 1, 1, yo, True, True))
+        ca, cb = copy(1, 0, 1, ev[0]), copy(2, 1, 1, ev[1])
+        need("g", ca, cb)
+        send((A0, "s%d" % ((k - n1 - 1) % 3), slot("so", 0), [(peer[0], slot("si", (k - n1 - 1) % 3))]),
+             (A1, "s%d" % ((k - n2 - 1) % 3), slot("so", 1), [(peer[1], slot("si", (k - n2 - 1) % 3))]))
+        Z(T2b), Z(T3)
+        R01(T2b), R23(T2b), Q(T2b)
+        O(T2b, (3, 0, 1, ev[2], True, True))
+        R01(T3, (0,))
+        cc = copy(3, 2, 1, ev[2])
+        R01(T3, (1,)), R23(T3), Q(T3)
+        O(T3, (1, 0, 2, ev[3], True, True), (2, 2, 1, ev[4], True, True))
+        need("g", cc)
+        send((allE, "s4", slot("so", 2), [(partner[far], slot("si", 4))]))
+        cd, ce = copy(1, 3, 2, ev[3]), copy(2, 5, 1, ev[4])
+        need("g", cd)
+        gn, gf = group[near], group[far]
+        s1, s2 = 2 + (k - n1 - 1) % 3, 2 + (k - n2 - 1) % 3
+        send((A0, "s%d" % s1, slot("so", 3), [(gn[n1], slot("si", s1))]),
+             (A1, "s%d" % s2, slot("so", 4), [(gn[n2], slot("si", s2))]))
+        need("g", ce)
+        send((allE, "s4", slot("so", 5), [(gn[k], slot("si", 4))]))
+        Z(T2a)
+        R01(T2a), R23(T2a), Q(T2a)
+        O(T2a, (3, 0, 2, ev[5], True, True))
+        cf = copy(3, 6, 2, ev[5])
+        need("g", cf)
+        send((A0, "s%d" % s1, slot("so", 6), [(gf[n1], slot("si", s1))]),
+             (A1, "s%d" % s2, slot("so", 7), [(gf[n2], slot("si", s2))]))
+        land = [(0, nE // 2), (1, nE // 2)] + [(2 + ends.index(h), nE) for h in (near, far)]
+    else:
+        L0 = batch([qx, qw], "s", X, "s", 0, 128, 0)
+        C0 = batch([at], "s", X, "t", 0, 128, 1)
+        C1 = batch([ap0], "a", 0, "t", 0, 128, 0)
+        C2 = batch([ap1], "a", W + 3 * X, "t", 0, 128, 1)
+        B2 = batch([qx2], "t", X, "a", W, 384, 0)
+        L1 = batch([], "a", 0, "s", 0, 128, 1)
+        L2 = batch([], "a", W + 3 * X, "s", 0, 128, 0)
+        c, o1, o2 = ev[0], ev[1], ev[2]
+        Z(L0), R01(L0), R23(L0), Q(L0)
+        O(L0, (0, 0, 1, yo, True, False))
+        Z(C0), R01(C0), R23(C0), Q(C0)
+        O(C0, (1, 0, 1, c, True, False))
+        Z(C1), R01(C1), R23(C1), Q(C1)
+        Z(C2), R01(C2), R23(C2), Q(C2)
+        O(C1, (1, 0, 1, c, False, False))
+        Z(B2, (0,))
+        O(C2, (1, 0, 1, c, False, True))
+        R01(B2, (0,))
+        cc = copy(1, 0, 1, c)
+        need("g", cc)
+        ms = "s%d" % (2 + ends.index(me))
+        send((allE, ms, slot("so", 0), [(t, slot("si", 2 + ends.index(me)))]))
+        Z(B2, (1,))
+        R01(B2, (1,)), R23(B2), Q(B2)
+        Z(L1), R01(L1), R23(L1), Q(L1)
+        O(B2, (2, 0, 1, o1, True, True), (3, 2, 1, o2, True, True), (0, 1, 1, yo, False, False))
+        ca, cb = copy(2, 1, 1, o1), copy(3, 2, 1, o2)
+        need("g", ca, cb)
+        s1, s2 = (k - n1 - 1) % 3, (k - n2 - 1) % 3
+        send((A0, "s%d" % s1, slot("so", 1), [(p1, slot("si", s1))]),
+             (A1, "s%d" % s2, slot("so", 2), [(p2, slot("si", s2))]))
+        Z(L2), R01(L2), R23(L2), Q(L2)
+        O(L1, (0, 0, 1, yo, False, False))
+        O(L2, (0, 0, 1, yo, False, True))
+        land = [(0, nE // 2), (1, nE // 2), (2, nE // 2), (3, nE // 2), (4, nE)]
+
+    last = None
+    need("V", yo)
+    for i, n in land:
+        nxt = event()
+        need("V", ["s%d" % i, n], last)
+        inc(g.vector.tensor_tensor(T.acc[:], T.po[:, 0:128] if last is None else T.acc[:], slot("si", i), AluOpType.add), nxt)
+        last = nxt
+    need("Y", last)
+    g.sync.dma_start(T.y[:], T.acc[:]).then_inc(T.sem["stored"], 16)
+    g.sync.wait_ge(T.sem["stored"], 16)
+    need("g", sent)

@@ -10,24 +10,27 @@ SCRATCH = {
     "xin": ("sbuf", [128, 512], BF), "w1in": ("sbuf", [128, 1024], BF), "w2in": ("sbuf", [128, 512], BF),
     "h": ("sbuf", [128, 4 * 1152], BF),
     "so": ("sbuf", [128, 8 * 128], F32),
-    "si": ("sbuf", [128, 8 * 128], F32),
+    "si": ("sbuf", [128, 5 * 128], F32),
     "acc": ("sbuf", [128, 128], F32),
     "pz": ("psum", [128, 2048], F32),
     "po": ("psum", [128, 2048], F32),
 }
-for _n, _w in (("s", 640),
+for _n, _w in (("s", 512),
                ("a", 1152),
                ("t", 512),
                ("m", 384),
-               ("f0", 768),
-               ("f1", 768),
+               ("n", 768),
+               ("f", 768),
                ("h", 1152)):
     SCRATCH["q" + _n] = ("sbuf", [128, _w], F8)
     SCRATCH["p" + _n] = ("sbuf", [128, _w], U8)
 
 EVENTS = 80
-SEMAPHORES = (["lx", "lw1", "lw2", "sent", "stored", "am", "ap0", "ap1", "at", "f0p", "f0x", "f1p", "f1x"]
-              + ["s%d" % i for i in range(8)] + ["e%d" % i for i in range(EVENTS)])
+SEMAPHORES = (["lx", "lw1", "lw2", "sent", "stored",
+               "mx",
+               "nw", "nx", "fw", "fx", "fy",
+               "px", "pw1", "pw2", "tw"]
+              + ["s%d" % i for i in range(5)] + ["e%d" % i for i in range(EVENTS)])
 
 
 def rank_program(g, core, T, topo):
@@ -37,11 +40,12 @@ def rank_program(g, core, T, topo):
     hosts = sorted({topo.host(c) for c in T.cores})
     group = {h: sorted((c for c in T.cores if topo.host(c) == h), key=topo.chip) for h in hosts}
     mid = [h for h in hosts if all(topo.may_write(a, b) for a in group[h] for b in T.cores if b != a)][0]
-    ends = [h for h in hosts if h != mid]
+    near = [h for h in hosts if h != mid and topo.same_plane(group[h][0], group[mid][0])][0]
+    far = [h for h in hosts if h not in (mid, near)][0]
     me = topo.host(core)
     k = group[me].index(core)
     n1, n2 = (k + 1) % 3, (k + 2) % 3
-    partner = {h: [c for c in group[h] if topo.chip(c) == topo.chip(core)][0] for h in hosts}
+    gm, gn, gf = group[mid], group[near], group[far]
 
     ev_n = [0]
 
@@ -49,24 +53,25 @@ def rank_program(g, core, T, topo):
         ev_n[0] += 1
         return ["e%d" % (ev_n[0] - 1), 0]
 
-    def inc(call, ev, n=1):
-        call.then_inc(T.sem[ev[0]], n)
-        ev[1] += n
+    def inc(call, ev):
+        call.then_inc(T.sem[ev[0]], 1)
+        ev[1] += 1
 
     queues = {"g": g, "T": g.tensor, "V": g.vector, "S": g.scalar, "Y": g.sync}
     waited = {q: {} for q in queues}
 
     def need(q, *evs):
         for ev in evs:
-            if ev is not None and waited[q].get(ev[0], 0) < ev[1]:
+            if waited[q].get(ev[0], 0) < ev[1]:
                 queues[q].wait_ge(T.sem[ev[0]], ev[1])
                 waited[q][ev[0]] = ev[1]
 
+    other = gn[k] if me == mid else gm[k]
+    m = topo.mask(core, other)
+    allE = [e for e in range(m.bit_length()) if (m >> e) & 1]
+    E0, E1 = allE[0::2], allE[1::2]
+    nE, hE = len(allE), len(allE) // 2
     sent = ["sent", 0]
-
-    def engines(dst):
-        m = topo.mask(core, dst)
-        return [e for e in range(m.bit_length()) if (m >> e) & 1]
 
     def send(*transfers):
         out = []
@@ -88,226 +93,164 @@ def rank_program(g, core, T, topo):
 
     def send_mx(*transfers):
         for view in (codes, scales):
-            send(*[(eng, sem, view("s", a, a + n), [(d, view(buf, b, b + n)) for d, buf, b in dests])
-                   for eng, sem, a, n, dests in transfers])
+            send(*[(eng, sem, view(src[0], src[1], src[1] + n), [(d, view(buf, b, b + n)) for d, buf, b in dests])
+                   for eng, sem, src, n, dests in transfers])
 
     def slot(buf, i, n=1):
         return T[buf][:, 128 * i:128 * (i + n)]
 
-    lx, lw1, lw2 = ["lx", 16], ["lw1", 16], ["lw2", 16]
     g.sync.dma_start(T.xin[:], T.x[:]).then_inc(T.sem["lx"], 16)
     g.scalar.dma_start(T.w1in[:], T.w1[:]).then_inc(T.sem["lw1"], 16)
     g.sync.dma_start(T.w2in[:], T.w2[:]).then_inc(T.sem["lw2"], 16)
 
-    def quantise(src, name, a, b, ev):
+    def quantise(load, src, name, a, b, ev):
+        need("V", [load, 16])
         inc(g.vector.quantize_mx(T["q" + name][:, a:b], T["p" + name][:, a:b], src[:]), ev)
 
     qx, qx2, qw = event(), event(), event()
-    need("V", lx)
-    quantise(T.xin, "s", 0, X, qx)
+    quantise("lx", T.xin, "s", 0, X, qx)
     if me == mid:
-        quantise(T.xin, "m", X, 2 * X, qx2)
+        quantise("lx", T.xin, "m", X, 2 * X, qx2)
     else:
-        quantise(T.xin, "s", X + W, 2 * X + W, qx2)
-        quantise(T.xin, "a", W + X, W + 2 * X, qx2)
-    need("V", lw1)
-    quantise(T.w1in, "s", X, X + 256, qw)
-    need("V", lw2)
-    quantise(T.w2in, "s", X + 256, X + W, qw)
+        quantise("lx", T.xin, "a", W + X, W + 2 * X, qx2)
+    quantise("lw1", T.w1in, "s", X, X + 256, qw)
+    quantise("lw2", T.w2in, "s", X + 256, X + W, qw)
 
+    def behind(j):
+        return (k - j - 1) % 3
+
+    need("g", qx)
     if me == mid:
-        allE = engines(partner[ends[0]])
-        racks = {h: topo.same_plane(core, partner[h]) for h in ends}
-        half = {True: allE[0::2], False: allE[1::2]}
-        need("g", qx)
-        send_mx((allE, "am", 0, X, [(group[mid][j], "m", 0 if (j + 1) % 3 == k else 2 * X) for j in (n1, n2)]))
+        send_mx((allE, "mx", ("s", 0), X, [(gm[j], "m", 2 * X * behind(j)) for j in (n1, n2)]))
         need("g", qw)
-        send_mx(*[(half[racks[h]], "at", 0, X + W, [(partner[h], "t", 0)]) for h in ends])
+        send_mx((E0, "tw", ("s", 0), X + W, [(gn[k], "t", 0)]), (E1, "tw", ("s", 0), X + W, [(gf[k], "t", 0)]))
+        need("g", ["fy", hE * 2])
+        send_mx((allE, "fx", ("f", 2 * X), X, [(gm[j], "f", X * behind(j)) for j in (n1, n2)]))
     else:
-        t = partner[mid]
-        fn = "f%d" % ends.index(me)
-        allE = engines(t)
-        toX = [(group[mid][j], fn, X * ((k - j - 1) % 3)) for j in (n1, n2)]
-        p1, p2 = group[me][n1], group[me][n2]
-        if topo.same_plane(core, t):
-            need("g", qx)
-            send_mx((allE, fn + "x", 0, X, toX))
+        t, p1, p2 = gm[k], group[me][n1], group[me][n2]
+        to_peers = [(p1, "a", W + 2 * X), (p2, "a", W)]
+        w_p1, w_p2 = ("pw2", ("s", X), W, [(p1, "a", W + 3 * X)]), ("pw1", ("s", X), W, [(p2, "a", 0)])
+        if me == near:
+            send_mx((allE, "px", ("s", 0), X, to_peers))
             need("g", qw)
-            send_mx((allE, fn + "p", 0, X + W, [(t, fn, 2 * X)]))
-            need("g", qx2)
-            send_mx((allE[0::2], "ap1", 0, X + W, [(p1, "a", W + 2 * X)]),
-                    (allE[1::2], "ap0", X, X + W, [(p2, "a", 0)]))
+            send_mx((allE, "nw", ("s", 0), X + W, [(t, "n", 2 * X)]))
+            send_mx((allE, "nx", ("s", 0), X, [(gm[j], "n", X * behind(j)) for j in (n1, n2)]))
+            send_mx((E0,) + w_p1, (E1,) + w_p2)
         else:
-            cab, sw = allE[1::2], allE[0::2]
-            need("g", qx, qx2, qw)
-            send_mx((cab, fn + "p", 0, X + W, [(t, fn, 2 * X)]),
-                    (sw[0::2], "ap1", 0, X + W, [(p1, "a", W + 2 * X)]),
-                    (sw[1::2], "ap0", X, X + W, [(p2, "a", 0)]))
-            send_mx((cab, fn + "x", 0, X, toX))
+            send_mx((E0, "px", ("s", 0), X, to_peers), (E1, "fy", ("s", 0), X, [(t, "f", 2 * X)]))
+            need("g", qw)
+            send_mx((E1, "fw", ("s", X), W, [(t, "f", 3 * X)]))
+            send_mx((E1,) + w_p1, (E0,) + w_p2)
 
-    nE = len(allE)
-    am = ["am", 2 * 2 * nE]
-    at = ["at", nE]
-    ap0, ap1 = ["ap0", nE], ["ap1", nE]
-    if me != mid and not topo.same_plane(core, partner[mid]):
-        ap0, ap1 = ["ap0", nE // 2], ["ap1", nE // 2]
-    fp, fx = {}, {}
-    for i, h in enumerate(ends):
-        near = topo.same_plane(partner[h], partner[mid])
-        fp[h] = ["f%dp" % i, 2 * nE if near else nE]
-        fx[h] = ["f%dx" % i, 2 * 2 * nE if near else 2 * nE]
-
-    zset = {0: [], 1: []}
-    bank_read = {}
-
-    off = [0]
-
-    def batch(need_ev, wbuf, w0, xbuf, x0, n, zs):
-        b = dict(arr=need_ev, w=(wbuf, w0), x=(xbuf, x0), n=n, zs=zs, off=off[0], z=[event(), event()],
-                 r=[event(), event()], q=event())
-        off[0] += n
-        return b
+    yo = event()
+    last_r, bank_ev, bank_read = {}, {0: yo}, {}
+    st = {"off": 0, "zs": 0, "pend": None}
 
     def mm(out, wname, w0, xname, x0, n, ev, start=True, stop=True):
         inc(g.tensor.matmul_mx(out, T["q" + wname][:, w0:w0 + 128], T["p" + wname][:, w0:w0 + 128],
                                T["q" + xname][:, x0:x0 + n], T["p" + xname][:, x0:x0 + n], start, stop), ev)
 
-    def Z(b, which=(0, 1)):
-        need("T", *b["arr"])
-        if 0 in which:
-            need("T", *zset[b["zs"]])
-        for i in which:
-            c0 = 512 * (2 * b["zs"] + i)
-            mm(T.pz[:, c0:c0 + b["n"]], b["w"][0], b["w"][1] + 128 * i, b["x"][0], b["x"][1], b["n"], b["z"][i])
-        zset[b["zs"]] = b["r"]
+    def finish():
+        if st["pend"] is None:
+            return
+        wbuf, w0, off, q, outs = st["pend"]
+        st["pend"] = None
+        need("T", q)
+        for bank, j, start, stop, _ in outs:
+            if start and bank:
+                if bank in bank_read:
+                    need("T", bank_read[bank])
+                bank_ev[bank] = event()
+            mm(T.po[:, 512 * bank:512 * bank + 128], wbuf, w0 + 256, "h", off + 128 * j, 128, bank_ev[bank], start, stop)
+        leave = []
+        for bank, _, _, _, to in outs:
+            if to is not None:
+                o, eng, dst, s = to
+                c = event()
+                need("S", bank_ev[bank])
+                inc(g.scalar.activation(slot("so", o), T.po[:, 512 * bank:512 * bank + 128], ActivationFunctionType.Copy), c)
+                bank_read[bank] = c
+                leave.append((c, (eng, "s%d" % s, slot("so", o), [(dst, slot("si", s))])))
+        if leave:
+            need("g", *[c for c, _ in leave])
+            send(*[tr for _, tr in leave])
 
-    def tile_view(b, i):
-        return T.h[:, 4 * b["off"] + i:4 * (b["off"] + b["n"]):4]
+    def batch(arrived, wbuf, w0, xbuf, x0, n, outs, alone=False):
+        if alone:
+            finish()
+        off, zs = st["off"], st["zs"]
+        st["off"], st["zs"] = off + n, 1 - zs
+        z, r, q = [event(), event()], [event(), event()], event()
+        need("T", *arrived)
+        need("T", *last_r.get(zs, []))
+        last_r[zs] = r
 
-    def R01(b, which=(0, 1)):
-        c0 = 512 * 2 * b["zs"]
-        need("S", b["z"][0])
-        for i in which:
-            inc(g.scalar.activation(tile_view(b, i), T.pz[:, c0:c0 + b["n"]], ActivationFunctionType.Relu,
-                                    scale=-C if i else C), b["r"][0])
+        def bank(b):
+            return T.pz[:, 512 * (2 * zs + b):512 * (2 * zs + b) + n]
 
-    def R23(b):
-        c0 = 512 * (2 * b["zs"] + 1)
-        need("V", b["z"][1])
-        for i in (0, 1):
-            inc(g.vector.tensor_scalar(tile_view(b, 2 + i), T.pz[:, c0:c0 + b["n"]], -C if i else C, 0.0,
-                                       AluOpType.mult, AluOpType.max), b["r"][1])
+        def rows(b):
+            return T.h[:, 4 * off + b:4 * (off + n):4]
 
-    def Q(b):
-        need("V", b["r"][0], b["r"][1])
-        a, e = b["off"], b["off"] + b["n"]
-        inc(g.vector.quantize_mx(T.qh[:, a:e], T.ph[:, a:e], T.h[:, 4 * a:4 * e]), b["q"])
+        for b in (0, 1):
+            mm(bank(b), wbuf, w0 + 128 * b, xbuf, x0, n, z[b])
+        need("S", z[0])
+        for b in (0, 1):
+            inc(g.scalar.activation(rows(b), bank(0), ActivationFunctionType.Relu, scale=-C if b else C), r[0])
+        need("V", z[1])
+        for b in (0, 1):
+            inc(g.vector.tensor_scalar(rows(2 + b), bank(1), -C if b else C, 0.0, AluOpType.mult, AluOpType.max), r[1])
+        need("V", *r)
+        inc(g.vector.quantize_mx(T.qh[:, off:off + n], T.ph[:, off:off + n], T.h[:, 4 * off:4 * (off + n)]), q)
+        finish()
+        st["pend"] = (wbuf, w0, off, q, outs)
 
-    def O(b, *outs):
-        need("T", b["q"])
-        for bank, i, m, ev, start, stop in outs:
-            if start:
-                need("T", bank_read.get(bank))
-            mm(T.po[:, 512 * bank:512 * bank + 128 * m], b["w"][0], b["w"][1] + 256, "h", b["off"] + 128 * i, 128 * m,
-               ev, start, stop)
-
-    def copy(bank, i, m, ev):
-        c = event()
-        need("S", ev)
-        inc(g.scalar.activation(slot("so", i, m), T.po[:, 512 * bank:512 * bank + 128 * m],
-                                ActivationFunctionType.Copy), c)
-        bank_read[bank] = c
-        return c
-
-    yo = event()
-    ev = [event() for _ in range(6)]
-    A0, A1 = allE[:nE // 2], allE[nE // 2:]
     if me == mid:
-        e0, e1 = ends
-        far, near = (e0, e1) if topo.same_plane(core, partner[e1]) else (e1, e0)
-        ff, fnr = "f%d" % ends.index(far), "f%d" % ends.index(near)
-        peer = [group[mid][n1], group[mid][n2]]
-        T1 = batch([qx2, qw, am], "s", X, "m", 0, 384, 0)
-        T2b = batch([fp[far], fp[near]], fnr, 3 * X, ff, 2 * X, 128, 1)
-        T3 = batch([fp[far], fx[near]], ff, 3 * X, fnr, 0, 384, 0)
-        T2a = batch([fx[far]], fnr, 3 * X, ff, 0, 256, 1)
-        Z(T1)
-        R01(T1), R23(T1), Q(T1)
-        O(T1, (1, 0, 1, ev[0], True, True), (2, 2, 1, ev[1], True, True), (0, 1, 1, yo, True, True))
-        ca, cb = copy(1, 0, 1, ev[0]), copy(2, 1, 1, ev[1])
-        need("g", ca, cb)
-        send((A0, "s%d" % ((k - n1 - 1) % 3), slot("so", 0), [(peer[0], slot("si", (k - n1 - 1) % 3))]),
-             (A1, "s%d" % ((k - n2 - 1) % 3), slot("so", 1), [(peer[1], slot("si", (k - n2 - 1) % 3))]))
-        Z(T2b), Z(T3)
-        R01(T2b), R23(T2b), Q(T2b)
-        O(T2b, (3, 0, 1, ev[2], True, True))
-        R01(T3, (0,))
-        cc = copy(3, 2, 1, ev[2])
-        R01(T3, (1,)), R23(T3), Q(T3)
-        O(T3, (1, 0, 2, ev[3], True, True), (2, 2, 1, ev[4], True, True))
-        need("g", cc)
-        send((allE, "s4", slot("so", 2), [(partner[far], slot("si", 4))]))
-        cd, ce = copy(1, 3, 2, ev[3]), copy(2, 5, 1, ev[4])
-        need("g", cd)
-        gn, gf = group[near], group[far]
-        s1, s2 = 2 + (k - n1 - 1) % 3, 2 + (k - n2 - 1) % 3
-        send((A0, "s%d" % s1, slot("so", 3), [(gn[n1], slot("si", s1))]),
-             (A1, "s%d" % s2, slot("so", 4), [(gn[n2], slot("si", s2))]))
-        need("g", ce)
-        send((allE, "s4", slot("so", 5), [(gn[k], slot("si", 4))]))
-        Z(T2a)
-        R01(T2a), R23(T2a), Q(T2a)
-        O(T2a, (3, 0, 2, ev[5], True, True))
-        cf = copy(3, 6, 2, ev[5])
-        need("g", cf)
-        send((A0, "s%d" % s1, slot("so", 6), [(gf[n1], slot("si", s1))]),
-             (A1, "s%d" % s2, slot("so", 7), [(gf[n2], slot("si", s2))]))
-        land = [(0, nE // 2), (1, nE // 2)] + [(2 + ends.index(h), nE) for h in (near, far)]
-    else:
-        L0 = batch([qx, qw], "s", X, "s", 0, 128, 0)
-        C0 = batch([at], "s", X, "t", 0, 128, 1)
-        C1 = batch([ap0], "a", 0, "t", 0, 128, 0)
-        C2 = batch([ap1], "a", W + 3 * X, "t", 0, 128, 1)
-        B2 = batch([qx2], "t", X, "a", W, 384, 0)
-        L1 = batch([], "a", 0, "s", 0, 128, 1)
-        L2 = batch([], "a", W + 3 * X, "s", 0, 128, 0)
-        c, o1, o2 = ev[0], ev[1], ev[2]
-        Z(L0), R01(L0), R23(L0), Q(L0)
-        O(L0, (0, 0, 1, yo, True, False))
-        Z(C0), R01(C0), R23(C0), Q(C0)
-        O(C0, (1, 0, 1, c, True, False))
-        Z(C1), R01(C1), R23(C1), Q(C1)
-        Z(C2), R01(C2), R23(C2), Q(C2)
-        O(C1, (1, 0, 1, c, False, False))
-        Z(B2, (0,))
-        O(C2, (1, 0, 1, c, False, True))
-        R01(B2, (0,))
-        cc = copy(1, 0, 1, c)
-        need("g", cc)
-        ms = "s%d" % (2 + ends.index(me))
-        send((allE, ms, slot("so", 0), [(t, slot("si", 2 + ends.index(me)))]))
-        Z(B2, (1,))
-        R01(B2, (1,)), R23(B2), Q(B2)
-        Z(L1), R01(L1), R23(L1), Q(L1)
-        O(B2, (2, 0, 1, o1, True, True), (3, 2, 1, o2, True, True), (0, 1, 1, yo, False, False))
-        ca, cb = copy(2, 1, 1, o1), copy(3, 2, 1, o2)
-        need("g", ca, cb)
-        s1, s2 = (k - n1 - 1) % 3, (k - n2 - 1) % 3
-        send((A0, "s%d" % s1, slot("so", 1), [(p1, slot("si", s1))]),
-             (A1, "s%d" % s2, slot("so", 2), [(p2, slot("si", s2))]))
-        Z(L2), R01(L2), R23(L2), Q(L2)
-        O(L1, (0, 0, 1, yo, False, False))
-        O(L2, (0, 0, 1, yo, False, True))
-        land = [(0, nE // 2), (1, nE // 2), (2, nE // 2), (3, nE // 2), (4, nE)]
+        mx, nw, nx = ["mx", 4 * nE], ["nw", 2 * nE], ["nx", 4 * nE]
+        fy, fw, fx = ["fy", 2 * hE], ["fw", 2 * hE], ["fx", 4 * nE]
 
-    last = None
-    need("V", yo)
-    for i, n in land:
-        nxt = event()
-        need("V", ["s%d" % i, n], last)
-        inc(g.vector.tensor_tensor(T.acc[:], T.po[:, 0:128] if last is None else T.acc[:], slot("si", i), AluOpType.add), nxt)
-        last = nxt
-    need("Y", last)
+        def out(bank, o, dst, s):
+            return [(bank, 0, True, True, (o, allE, dst, s))]
+
+        batch([qx2, qw, mx], "s", X, "m", 0, 384, [(1, 0, True, True, (0, E0, gm[n1], behind(n1))),
+                                                   (2, 2, True, True, (1, E1, gm[n2], behind(n2))), (0, 1, True, True, None)])
+        batch([nw, fy], "n", 3 * X, "f", 2 * X, 128, out(3, 2, gf[k], 4), alone=True)
+        batch([fw, nx], "f", 3 * X, "n", 0, 128, out(1, 3, gn[n1], 2 + behind(n1)))
+        batch([], "f", 3 * X, "n", X, 128, out(2, 4, gn[n2], 2 + behind(n2)))
+        batch([], "f", 3 * X, "n", 2 * X, 128, out(1, 5, gn[k], 4))
+        batch([fx], "n", 3 * X, "f", 0, 128, out(3, 6, gf[n1], 2 + behind(n1)), alone=True)
+        batch([], "n", 3 * X, "f", X, 128, out(2, 7, gf[n2], 2 + behind(n2)))
+        finish()
+        land = [(0, hE), (1, hE), (2, nE), (3, nE)]
+    else:
+        px = ["px", 2 * 2 * (nE if me == near else hE)]
+        tw, pw1, pw2 = ["tw", 2 * hE], ["pw1", 2 * hE], ["pw2", 2 * hE]
+        to_t = (0, allE, t, 2 if me == near else 3)
+        w1p, w2p = ("a", 0), ("a", W + 3 * X)
+        batch([qx, qw], "s", X, "s", 0, 128, [(0, 0, True, False, None)])
+        batch([tw], "s", X, "t", 0, 128, [(1, 0, True, False, None)], alone=True)
+        batch([px, qx2], "t", X, "a", W, 384, [(2, 0, True, True, (1, E0, p1, behind(n1))),
+                                               (3, 2, True, True, (2, E1, p2, behind(n2))), (0, 1, False, False, None)], alone=True)
+        batch([pw1], *w1p, "t", 0, 128, [(1, 0, False, False, None)], alone=True)
+        batch([pw2], *w2p, "t", 0, 128, [(1, 0, False, True, to_t)])
+        batch([], *w1p, "s", 0, 128, [(0, 0, False, False, None)])
+        batch([], *w2p, "s", 0, 128, [(0, 0, False, True, None)])
+        finish()
+        land = [(0, hE), (1, hE), (2, nE), (3, nE), (4, nE)]
+
+    (s0, c0), rest = land[0], land[1:]
+    need("V", ["s%d" % s0, c0])
+    a, last = slot("si", s0), None
+    for s, n in rest:
+        need("V", ["s%d" % s, n])
+        if last is not None:
+            need("V", last)
+        last = event()
+        inc(g.vector.tensor_tensor(T.acc[:], a, slot("si", s), AluOpType.add), last)
+        a = T.acc[:]
+    fin = event()
+    need("V", yo, last)
+    inc(g.vector.tensor_tensor(T.acc[:], T.po[:, 0:128], T.acc[:], AluOpType.add), fin)
+    need("Y", fin)
     g.sync.dma_start(T.y[:], T.acc[:]).then_inc(T.sem["stored"], 16)
     g.sync.wait_ge(T.sem["stored"], 16)
     need("g", sent)

@@ -3,49 +3,98 @@ from concourse.bass import DstId, RemoteDMATransfer
 from concourse.mybir import dt, AluOpType, ActivationFunctionType
 
 C = float(np.float32(0.047))
+WORLD = 512
 X, W = 128, 384
 F8, U8, BF, F32 = "float8_e4m3fn_x4", "uint8", "bfloat16", "float32"
 
 SCRATCH = {
     "xin": ("sbuf", [128, 512], BF), "w1in": ("sbuf", [128, 1024], BF), "w2in": ("sbuf", [128, 512], BF),
     "h": ("sbuf", [128, 4 * 1152], BF),
-    "so": ("sbuf", [128, 8 * 128], F32),
-    "si": ("sbuf", [128, 5 * 128], F32),
-    "acc": ("sbuf", [128, 128], F32),
+    "so": ("sbuf", [128, 2 * 128], F32),
+    "si": ("sbuf", [128, 2 * 128], F32),
+    "acc": ("sbuf", [128, 2 * 128], F32),
     "pz": ("psum", [128, 2048], F32),
-    "po": ("psum", [128, 2048], F32),
+    "po": ("psum", [128, 1536], F32),
 }
-for _n, _w in (("s", 512),
-               ("a", 1152),
-               ("t", 512),
-               ("m", 384),
-               ("n", 768),
-               ("f", 768),
+for _n, _w in (("x", 3 * X),
+               ("w", 3 * W),
                ("h", 1152)):
     SCRATCH["q" + _n] = ("sbuf", [128, _w], F8)
     SCRATCH["p" + _n] = ("sbuf", [128, _w], U8)
 
-EVENTS = 80
+EVENTS = 60
 SEMAPHORES = (["lx", "lw1", "lw2", "sent", "stored",
-               "mx",
-               "nw", "nx", "fw", "fx", "fy",
-               "px", "pw1", "pw2", "tw"]
-              + ["s%d" % i for i in range(5)] + ["e%d" % i for i in range(EVENTS)])
+               "x0", "x1", "w1", "w2", "s0", "s1",
+               "rc", "rp", "rs"]
+              + ["e%d" % i for i in range(EVENTS)])
 
 
 def rank_program(g, core, T, topo):
-    if T.rank_of(core) is None:
-        return
-
     hosts = sorted({topo.host(c) for c in T.cores})
+    if T.rank_of(core) is None and topo.host(core) in hosts:
+        return
     group = {h: sorted((c for c in T.cores if topo.host(c) == h), key=topo.chip) for h in hosts}
     mid = [h for h in hosts if all(topo.may_write(a, b) for a in group[h] for b in T.cores if b != a)][0]
-    near = [h for h in hosts if h != mid and topo.same_plane(group[h][0], group[mid][0])][0]
-    far = [h for h in hosts if h not in (mid, near)][0]
+    near, far = sorted((h for h in hosts if h != mid), key=lambda h: not topo.same_plane(group[h][0], group[mid][0]))
+
+    def partners(c):
+        k = group[topo.host(c)].index(c)
+        return [group[h][k] for h in {mid: (far, near), near: (far, mid), far: (near, mid)}[topo.host(c)]]
+
+    def relays(k):
+        a, b = group[near][k], group[far][k]
+        out = [c for c in range(WORLD) if topo.host(c) not in hosts and topo.chip(c) == topo.chip(a)
+               and topo.die(c) == topo.die(a)
+               and all(topo.may_write(c, d) and topo.may_write(d, c) for d in (a, b))]
+        return {a: out[0], b: out[1]}
+
+    sent = ["sent", 0]
+
+    def engines(dst):
+        m = topo.mask(core, dst)
+        return [e for e in range(m.bit_length()) if (m >> e) & 1]
+
+    def send(*transfers):
+        out = []
+        for eng, sem, src, d, dst in transfers:
+            rid, pid = topo.addr(d, core)
+            out.append(RemoteDMATransfer(dst_ids=[DstId(rid=rid, pnc=pid)], dma_engine_mask=sum(1 << e for e in eng),
+                                         remote_sem=T.sem[sem], srcs=[src], dsts=[dst]))
+            sent[1] += len(eng)
+        g.remote_dma_fused(out, local_sem=T.sem["sent"])
+
+    def codes(name, a, b):
+        return T["q" + name][:, a:b].bitcast(dt.uint8)
+
+    def scales(name, a, b):
+        return T["p" + name][:, a:b]
+
+    def slot(buf, i):
+        return T[buf][:, 128 * i:128 * (i + 1)]
+
+    if T.rank_of(core) is None:
+        for k in range(len(group[near])):
+            r = relays(k)
+            for src, dst in ((group[near][k], group[far][k]), (group[far][k], group[near][k])):
+                if r[src] == core:
+                    s = partners(dst).index(src)
+                    eng, n_in = engines(dst), len(engines(dst))
+                    g.wait_ge(T.sem["rc"], n_in // 2)
+                    send((eng, "x%d" % s, codes("x", 0, X), dst, codes("x", X * s, X * s + X)))
+                    g.wait_ge(T.sem["rp"], n_in // 2)
+                    send((eng, "x%d" % s, scales("x", 0, X), dst, scales("x", X * s, X * s + X)))
+                    g.wait_ge(T.sem["rs"], n_in)
+                    send((eng, "s%d" % s, slot("si", 0), dst, slot("si", s)))
+                    g.wait_ge(T.sem["sent"], sent[1])
+        return
+
     me = topo.host(core)
     k = group[me].index(core)
-    n1, n2 = (k + 1) % 3, (k + 2) % 3
-    gm, gn, gf = group[mid], group[near], group[far]
+    p1, p2 = group[me][(k + 1) % 3], group[me][(k + 2) % 3]
+    part = partners(core)
+    allE = engines(p1)
+    E0, E1 = allE[0::2], allE[1::2]
+    nE, hE = len(allE), len(allE) // 2
 
     ev_n = [0]
 
@@ -66,39 +115,6 @@ def rank_program(g, core, T, topo):
                 queues[q].wait_ge(T.sem[ev[0]], ev[1])
                 waited[q][ev[0]] = ev[1]
 
-    other = gn[k] if me == mid else gm[k]
-    m = topo.mask(core, other)
-    allE = [e for e in range(m.bit_length()) if (m >> e) & 1]
-    E0, E1 = allE[0::2], allE[1::2]
-    nE, hE = len(allE), len(allE) // 2
-    sent = ["sent", 0]
-
-    def send(*transfers):
-        out = []
-        for eng, sem, src, dests in transfers:
-            ids = []
-            for d, _ in dests:
-                rid, pid = topo.addr(d, core)
-                ids.append(DstId(rid=rid, pnc=pid))
-            out.append(RemoteDMATransfer(dst_ids=ids, dma_engine_mask=sum(1 << e for e in eng), remote_sem=T.sem[sem],
-                                         srcs=[src], dsts=[v for _, v in dests]))
-            sent[1] += len(eng)
-        g.remote_dma_fused(out, local_sem=T.sem["sent"])
-
-    def codes(name, a, b):
-        return T["q" + name][:, a:b].bitcast(dt.uint8)
-
-    def scales(name, a, b):
-        return T["p" + name][:, a:b]
-
-    def send_mx(*transfers):
-        for view in (codes, scales):
-            send(*[(eng, sem, view(src[0], src[1], src[1] + n), [(d, view(buf, b, b + n)) for d, buf, b in dests])
-                   for eng, sem, src, n, dests in transfers])
-
-    def slot(buf, i, n=1):
-        return T[buf][:, 128 * i:128 * (i + n)]
-
     g.sync.dma_start(T.xin[:], T.x[:]).then_inc(T.sem["lx"], 16)
     g.scalar.dma_start(T.w1in[:], T.w1[:]).then_inc(T.sem["lw1"], 16)
     g.sync.dma_start(T.w2in[:], T.w2[:]).then_inc(T.sem["lw2"], 16)
@@ -107,77 +123,60 @@ def rank_program(g, core, T, topo):
         need("V", [load, 16])
         inc(g.vector.quantize_mx(T["q" + name][:, a:b], T["p" + name][:, a:b], src[:]), ev)
 
-    qx, qx2, qw = event(), event(), event()
-    quantise("lx", T.xin, "s", 0, X, qx)
-    if me == mid:
-        quantise("lx", T.xin, "m", X, 2 * X, qx2)
-    else:
-        quantise("lx", T.xin, "a", W + X, W + 2 * X, qx2)
-    quantise("lw1", T.w1in, "s", X, X + 256, qw)
-    quantise("lw2", T.w2in, "s", X + 256, X + W, qw)
+    qx, qw = event(), event()
+    quantise("lx", T.xin, "x", 2 * X, 3 * X, qx)
+    quantise("lw1", T.w1in, "w", 0, 256, qw)
+    quantise("lw2", T.w2in, "w", 256, W, qw)
 
-    def behind(j):
-        return (k - j - 1) % 3
+    def x_to(view, i, eng):
+        d = part[i]
+        if topo.may_write(core, d):
+            s = partners(d).index(core)
+            return (eng, "x%d" % s, view("x", 2 * X, 3 * X), d, view("x", X * s, X * s + X))
+        return (eng, "rc" if view is codes else "rp", view("x", 2 * X, 3 * X), relays(k)[core], view("x", 0, X))
 
     need("g", qx)
-    if me == mid:
-        send_mx((allE, "mx", ("s", 0), X, [(gm[j], "m", 2 * X * behind(j)) for j in (n1, n2)]))
-        need("g", qw)
-        send_mx((E0, "tw", ("s", 0), X + W, [(gn[k], "t", 0)]), (E1, "tw", ("s", 0), X + W, [(gf[k], "t", 0)]))
-        need("g", ["fy", hE * 2])
-        send_mx((allE, "fx", ("f", 2 * X), X, [(gm[j], "f", X * behind(j)) for j in (n1, n2)]))
-    else:
-        t, p1, p2 = gm[k], group[me][n1], group[me][n2]
-        to_peers = [(p1, "a", W + 2 * X), (p2, "a", W)]
-        w_p1, w_p2 = ("pw2", ("s", X), W, [(p1, "a", W + 3 * X)]), ("pw1", ("s", X), W, [(p2, "a", 0)])
-        if me == near:
-            send_mx((allE, "px", ("s", 0), X, to_peers))
-            need("g", qw)
-            send_mx((allE, "nw", ("s", 0), X + W, [(t, "n", 2 * X)]))
-            send_mx((allE, "nx", ("s", 0), X, [(gm[j], "n", X * behind(j)) for j in (n1, n2)]))
-            send_mx((E0,) + w_p1, (E1,) + w_p2)
-        else:
-            send_mx((E0, "px", ("s", 0), X, to_peers), (E1, "fy", ("s", 0), X, [(t, "f", 2 * X)]))
-            need("g", qw)
-            send_mx((E1, "fw", ("s", X), W, [(t, "f", 3 * X)]))
-            send_mx((E1,) + w_p1, (E0,) + w_p2)
+    for view in (codes, scales):
+        send(x_to(view, 0, E1), x_to(view, 1, E0))
+    need("g", qw)
+    for i, d in ((1, p1), (2, p2)):
+        for view in (codes, scales):
+            send((allE, "w%d" % i, view("w", 0, W), d, view("w", W * i, W * i + W)))
 
-    yo = event()
-    last_r, bank_ev, bank_read = {}, {0: yo}, {}
-    st = {"off": 0, "zs": 0, "pend": None}
+    last_r = {}
+    col = [event(), event(), event()]
+    st = {"off": 0, "zs": 0, "pend": None, "terms": [0, 0, 0]}
 
-    def mm(out, wname, w0, xname, x0, n, ev, start=True, stop=True):
-        inc(g.tensor.matmul_mx(out, T["q" + wname][:, w0:w0 + 128], T["p" + wname][:, w0:w0 + 128],
+    def mm(out, w0, xname, x0, n, ev, start=True, stop=True):
+        inc(g.tensor.matmul_mx(out, T["qw"][:, w0:w0 + 128], T["pw"][:, w0:w0 + 128],
                                T["q" + xname][:, x0:x0 + n], T["p" + xname][:, x0:x0 + n], start, stop), ev)
 
     def finish():
         if st["pend"] is None:
             return
-        wbuf, w0, off, q, outs = st["pend"]
+        w, c0, c1, off, q = st["pend"]
         st["pend"] = None
         need("T", q)
-        for bank, j, start, stop, _ in outs:
-            if start and bank:
-                if bank in bank_read:
-                    need("T", bank_read[bank])
-                bank_ev[bank] = event()
-            mm(T.po[:, 512 * bank:512 * bank + 128], wbuf, w0 + 256, "h", off + 128 * j, 128, bank_ev[bank], start, stop)
-        leave = []
-        for bank, _, _, _, to in outs:
-            if to is not None:
-                o, eng, dst, s = to
-                c = event()
-                need("S", bank_ev[bank])
-                inc(g.scalar.activation(slot("so", o), T.po[:, 512 * bank:512 * bank + 128], ActivationFunctionType.Copy), c)
-                bank_read[bank] = c
-                leave.append((c, (eng, "s%d" % s, slot("so", o), [(dst, slot("si", s))])))
-        if leave:
-            need("g", *[c for c, _ in leave])
-            send(*[tr for _, tr in leave])
+        for c in range(c0, c1):
+            n = st["terms"][c]
+            st["terms"][c] += 1
+            mm(T.po[:, 512 * c:512 * c + 128], W * w + 256, "h", off + 128 * (c - c0), 128, col[c], n == 0, n == 2)
+            if n == 2 and c < 2:
+                need("S", col[c])
+                out = event()
+                inc(g.scalar.activation(slot("so", c), T.po[:, 512 * c:512 * c + 128], ActivationFunctionType.Copy), out)
+                need("g", out)
+                d = part[c]
+                if topo.may_write(core, d):
+                    s = partners(d).index(core)
+                    send((allE, "s%d" % s, slot("so", c), d, slot("si", s)))
+                else:
+                    send((allE, "rs", slot("so", c), relays(k)[core], slot("si", 0)))
 
-    def batch(arrived, wbuf, w0, xbuf, x0, n, outs, alone=False):
+    def batch(arrived, w, c0, c1, alone=False, hurry=False):
         if alone:
             finish()
+        n = X * (c1 - c0)
         off, zs = st["off"], st["zs"]
         st["off"], st["zs"] = off + n, 1 - zs
         z, r, q = [event(), event()], [event(), event()], event()
@@ -192,7 +191,9 @@ def rank_program(g, core, T, topo):
             return T.h[:, 4 * off + b:4 * (off + n):4]
 
         for b in (0, 1):
-            mm(bank(b), wbuf, w0 + 128 * b, xbuf, x0, n, z[b])
+            mm(bank(b), W * w + 128 * b, "x", X * c0, n, z[b])
+        if hurry:
+            finish()
         need("S", z[0])
         for b in (0, 1):
             inc(g.scalar.activation(rows(b), bank(0), ActivationFunctionType.Relu, scale=-C if b else C), r[0])
@@ -202,55 +203,26 @@ def rank_program(g, core, T, topo):
         need("V", *r)
         inc(g.vector.quantize_mx(T.qh[:, off:off + n], T.ph[:, off:off + n], T.h[:, 4 * off:4 * (off + n)]), q)
         finish()
-        st["pend"] = (wbuf, w0, off, q, outs)
+        st["pend"] = (w, c0, c1, off, q)
 
-    if me == mid:
-        mx, nw, nx = ["mx", 4 * nE], ["nw", 2 * nE], ["nx", 4 * nE]
-        fy, fw, fx = ["fy", 2 * hE], ["fw", 2 * hE], ["fx", 4 * nE]
+    x_in = [["x%d" % i, 2 * (hE if topo.may_write(core, part[i]) else nE)] for i in (0, 1)]
+    w_in = [None, ["w1", 2 * nE], ["w2", 2 * nE]]
+    batch([qx, qw], 0, 2, 3)
+    batch([x_in[1]], 0, 1, 2, alone=True)
+    batch([w_in[1]], 1, 1, 3, alone=True)
+    batch([x_in[0]], 0, 0, 1, alone=True)
+    batch([], 1, 0, 1)
+    batch([w_in[2]], 2, 0, 1, alone=True)
+    batch([], 2, 1, 2, hurry=True)
+    batch([], 2, 2, 3, hurry=True)
+    finish()
 
-        def out(bank, o, dst, s):
-            return [(bank, 0, True, True, (o, allE, dst, s))]
-
-        batch([qx2, qw, mx], "s", X, "m", 0, 384, [(1, 0, True, True, (0, E0, gm[n1], behind(n1))),
-                                                   (2, 2, True, True, (1, E1, gm[n2], behind(n2))), (0, 1, True, True, None)])
-        batch([nw, fy], "n", 3 * X, "f", 2 * X, 128, out(3, 2, gf[k], 4), alone=True)
-        batch([fw, nx], "f", 3 * X, "n", 0, 128, out(1, 3, gn[n1], 2 + behind(n1)))
-        batch([], "f", 3 * X, "n", X, 128, out(2, 4, gn[n2], 2 + behind(n2)))
-        batch([], "f", 3 * X, "n", 2 * X, 128, out(1, 5, gn[k], 4))
-        batch([fx], "n", 3 * X, "f", 0, 128, out(3, 6, gf[n1], 2 + behind(n1)), alone=True)
-        batch([], "n", 3 * X, "f", X, 128, out(2, 7, gf[n2], 2 + behind(n2)))
-        finish()
-        land = [(0, hE), (1, hE), (2, nE), (3, nE)]
-    else:
-        px = ["px", 2 * 2 * (nE if me == near else hE)]
-        tw, pw1, pw2 = ["tw", 2 * hE], ["pw1", 2 * hE], ["pw2", 2 * hE]
-        to_t = (0, allE, t, 2 if me == near else 3)
-        w1p, w2p = ("a", 0), ("a", W + 3 * X)
-        batch([qx, qw], "s", X, "s", 0, 128, [(0, 0, True, False, None)])
-        batch([tw], "s", X, "t", 0, 128, [(1, 0, True, False, None)], alone=True)
-        batch([px, qx2], "t", X, "a", W, 384, [(2, 0, True, True, (1, E0, p1, behind(n1))),
-                                               (3, 2, True, True, (2, E1, p2, behind(n2))), (0, 1, False, False, None)], alone=True)
-        batch([pw1], *w1p, "t", 0, 128, [(1, 0, False, False, None)], alone=True)
-        batch([pw2], *w2p, "t", 0, 128, [(1, 0, False, True, to_t)])
-        batch([], *w1p, "s", 0, 128, [(0, 0, False, False, None)])
-        batch([], *w2p, "s", 0, 128, [(0, 0, False, True, None)])
-        finish()
-        land = [(0, hE), (1, hE), (2, nE), (3, nE), (4, nE)]
-
-    (s0, c0), rest = land[0], land[1:]
-    need("V", ["s%d" % s0, c0])
-    a, last = slot("si", s0), None
-    for s, n in rest:
-        need("V", ["s%d" % s, n])
-        if last is not None:
-            need("V", last)
-        last = event()
-        inc(g.vector.tensor_tensor(T.acc[:], a, slot("si", s), AluOpType.add), last)
-        a = T.acc[:]
-    fin = event()
-    need("V", yo, last)
-    inc(g.vector.tensor_tensor(T.acc[:], T.po[:, 0:128], T.acc[:], AluOpType.add), fin)
+    first, fin = event(), event()
+    need("V", col[2], ["s1", nE])
+    inc(g.vector.tensor_tensor(slot("acc", 0), T.po[:, 1024:1152], slot("si", 1), AluOpType.add), first)
+    need("V", first, ["s0", nE])
+    inc(g.vector.tensor_tensor(slot("acc", 1), slot("acc", 0), slot("si", 0), AluOpType.add), fin)
     need("Y", fin)
-    g.sync.dma_start(T.y[:], T.acc[:]).then_inc(T.sem["stored"], 16)
+    g.sync.dma_start(T.y[:], slot("acc", 1)).then_inc(T.sem["stored"], 16)
     g.sync.wait_ge(T.sem["stored"], 16)
     need("g", sent)

@@ -7,6 +7,19 @@ WORLD = 512
 X, W = 128, 384
 F8, U8, BF, F32 = "float8_e4m3fn_x4", "uint8", "bfloat16", "float32"
 
+SENDS = [("x", "c", [[("x0", "off"), ("h", "on")]]),
+         ("x", "p", [[("x0", "off"), ("h", "on")]]),
+         ("w", "c", [[("w1", "off"), ("h", "on")]]),
+         ("w", "p", [[("w1", "off")], [("w2", "off")]])]
+HELPER = [("x", "c", [[("x1", "off")]]),
+          ("x", "p", [[("x1", "off")]]),
+          ("w", "c", [[("w2", "off")]])]
+
+BATCHES = [(0, 2, 3), (0, 1, 2), (1, 1, 3), (0, 0, 1), (1, 0, 1), (2, 0, 1), (2, 1, 3)]
+TENSOR = "z0 o0 z1 z2 z3 o1 z4 z5 o2 o3 z6 o4 o5 o6".split()
+SCALAR = "a0 a1 a2 a3 a4 a5 a6 c0 c1".split()
+VECTOR = "t0 q0 t1 q1 t2 t3 q2 q3 t4 t5 q4 q5 t6 q6".split()
+
 SCRATCH = {
     "xin": ("sbuf", [128, 512], BF), "w1in": ("sbuf", [128, 1024], BF), "w2in": ("sbuf", [128, 512], BF),
     "h": ("sbuf", [128, 4 * 1152], BF),
@@ -25,17 +38,19 @@ for _n, _w in (("x", 3 * X),
 EVENTS = 60
 SEMAPHORES = (["lx", "lw1", "lw2", "sent", "stored",
                "x0", "x1", "w1", "w2", "s0", "s1",
-               "rc", "rp", "rs"]
+               "xc", "xp", "wc", "wp", "rs"]
               + ["e%d" % i for i in range(EVENTS)])
 
 
 def rank_program(g, core, T, topo):
     hosts = sorted({topo.host(c) for c in T.cores})
-    if T.rank_of(core) is None and topo.host(core) in hosts:
-        return
     group = {h: sorted((c for c in T.cores if topo.host(c) == h), key=topo.chip) for h in hosts}
     mid = [h for h in hosts if all(topo.may_write(a, b) for a in group[h] for b in T.cores if b != a)][0]
     near, far = sorted((h for h in hosts if h != mid), key=lambda h: not topo.same_plane(group[h][0], group[mid][0]))
+
+    def helper(c):
+        return [e for e in range(WORLD) if topo.host(e) == topo.host(c) and topo.chip(e) == topo.chip(c)
+                and topo.die(e) != topo.die(c)][0]
 
     def partners(c):
         k = group[topo.host(c)].index(c)
@@ -48,19 +63,22 @@ def rank_program(g, core, T, topo):
                and all(topo.may_write(c, d) and topo.may_write(d, c) for d in (a, b))]
         return {a: out[0], b: out[1]}
 
-    sent = ["sent", 0]
-
-    def engines(dst):
-        m = topo.mask(core, dst)
+    def bits(m):
         return [e for e in range(m.bit_length()) if (m >> e) & 1]
+
+    a, b = group[mid][:2]
+    ENG = {"off": bits(topo.mask(a, b))}
+    ENG["on"] = [e for e in bits(topo.mask(a, helper(a))) if e not in ENG["off"]]
+    nE = len(ENG["off"])
+    sent = ["sent", 0]
 
     def send(*transfers):
         out = []
         for eng, sem, src, d, dst in transfers:
             rid, pid = topo.addr(d, core)
-            out.append(RemoteDMATransfer(dst_ids=[DstId(rid=rid, pnc=pid)], dma_engine_mask=sum(1 << e for e in eng),
+            out.append(RemoteDMATransfer(dst_ids=[DstId(rid=rid, pnc=pid)], dma_engine_mask=sum(1 << e for e in ENG[eng]),
                                          remote_sem=T.sem[sem], srcs=[src], dsts=[dst]))
-            sent[1] += len(eng)
+            sent[1] += len(ENG[eng])
         g.remote_dma_fused(out, local_sem=T.sem["sent"])
 
     def codes(name, a, b):
@@ -69,8 +87,27 @@ def rank_program(g, core, T, topo):
     def scales(name, a, b):
         return T["p" + name][:, a:b]
 
+    VIEW = {"c": codes, "p": scales}
+    WIDTH = {"x": X, "w": W}
+
     def slot(buf, i):
         return T[buf][:, 128 * i:128 * (i + 1)]
+
+    def landing(target, v=None):
+        return sum(len(ENG[e]) for _, w, calls in SENDS + HELPER if v in (None, w) for call in calls for t, e in call if t == target)
+
+    def goes(owner, what, v, target, eng, src):
+        view, k = VIEW[v], group[topo.host(owner)].index(owner)
+        if target == "h":
+            return (eng, what + v, src, helper(owner), view(what, 0, WIDTH[what]))
+        i = int(target[1])
+        if what == "w":
+            return (eng, target, src, group[topo.host(owner)][(k + i) % 3], view("w", W * i, W * i + W))
+        d = partners(owner)[i]
+        if topo.may_write(owner, d):
+            s = partners(d).index(owner)
+            return (eng, "x%d" % s, src, d, view("x", X * s, X * s + X))
+        return (eng, "x" + v, src, relays(k)[owner], view("x", 0, X))
 
     if T.rank_of(core) is None:
         for k in range(len(group[near])):
@@ -78,149 +115,139 @@ def rank_program(g, core, T, topo):
             for src, dst in ((group[near][k], group[far][k]), (group[far][k], group[near][k])):
                 if r[src] == core:
                     s = partners(dst).index(src)
-                    eng, n_in = engines(dst), len(engines(dst))
-                    g.wait_ge(T.sem["rc"], n_in // 2)
-                    send((eng, "x%d" % s, codes("x", 0, X), dst, codes("x", X * s, X * s + X)))
-                    g.wait_ge(T.sem["rp"], n_in // 2)
-                    send((eng, "x%d" % s, scales("x", 0, X), dst, scales("x", X * s, X * s + X)))
-                    g.wait_ge(T.sem["rs"], n_in)
-                    send((eng, "s%d" % s, slot("si", 0), dst, slot("si", s)))
+                    for v in "cp":
+                        g.wait_ge(T.sem["x" + v], landing("x0", v))
+                        send(("off", "x%d" % s, VIEW[v]("x", 0, X), dst, VIEW[v]("x", X * s, X * s + X)))
+                    g.wait_ge(T.sem["rs"], nE)
+                    send(("off", "s%d" % s, slot("si", 0), dst, slot("si", s)))
                     g.wait_ge(T.sem["sent"], sent[1])
+        for owner in T.cores:
+            if helper(owner) == core:
+                for what, v, calls in HELPER:
+                    g.wait_ge(T.sem[what + v], sum(len(ENG[e]) for k, w, cs in SENDS if (k, w) == (what, v)
+                                                   for call in cs for t, e in call if t == "h"))
+                    for call in calls:
+                        send(*[goes(owner, what, v, t, e, VIEW[v](what, 0, WIDTH[what])) for t, e in call])
+                g.wait_ge(T.sem["sent"], sent[1])
         return
 
     me = topo.host(core)
     k = group[me].index(core)
-    p1, p2 = group[me][(k + 1) % 3], group[me][(k + 2) % 3]
     part = partners(core)
-    allE = engines(p1)
-    E0, E1 = allE[0::2], allE[1::2]
-    nE, hE = len(allE), len(allE) // 2
 
     ev_n = [0]
 
-    def event():
+    def event(n=1):
         ev_n[0] += 1
-        return ["e%d" % (ev_n[0] - 1), 0]
+        return ("e%d" % (ev_n[0] - 1), n)
 
     def inc(call, ev):
         call.then_inc(T.sem[ev[0]], 1)
-        ev[1] += 1
 
     queues = {"g": g, "T": g.tensor, "V": g.vector, "S": g.scalar, "Y": g.sync}
-    waited = {q: {} for q in queues}
+    waited = {q: set() for q in queues}
 
     def need(q, *evs):
         for ev in evs:
-            if waited[q].get(ev[0], 0) < ev[1]:
+            if ev[0] not in waited[q]:
                 queues[q].wait_ge(T.sem[ev[0]], ev[1])
-                waited[q][ev[0]] = ev[1]
+                waited[q].add(ev[0])
 
-    g.sync.dma_start(T.xin[:], T.x[:]).then_inc(T.sem["lx"], 16)
-    g.scalar.dma_start(T.w1in[:], T.w1[:]).then_inc(T.sem["lw1"], 16)
-    g.sync.dma_start(T.w2in[:], T.w2[:]).then_inc(T.sem["lw2"], 16)
+    for name in ("x", "w1", "w2"):
+        g.sync.dma_start(T[name + "in"][:], T[name][:]).then_inc(T.sem["l" + name], 16)
+    qx, qw = event(), event(2)
+    for name, to, c0, c1, ev in (("x", "x", 2 * X, 3 * X, qx), ("w1", "w", 0, 256, qw), ("w2", "w", 256, W, qw)):
+        need("V", ("l" + name, 16))
+        inc(g.vector.quantize_mx(T["q" + to][:, c0:c1], T["p" + to][:, c0:c1], T[name + "in"][:]), ev)
 
-    def quantise(load, src, name, a, b, ev):
-        need("V", [load, 16])
-        inc(g.vector.quantize_mx(T["q" + name][:, a:b], T["p" + name][:, a:b], src[:]), ev)
+    for what, v, calls in SENDS:
+        need("g", qx if what == "x" else qw)
+        src = VIEW[v]("x", 2 * X, 3 * X) if what == "x" else VIEW[v]("w", 0, W)
+        for call in calls:
+            send(*[goes(core, what, v, t, e, src) for t, e in call])
 
-    qx, qw = event(), event()
-    quantise("lx", T.xin, "x", 2 * X, 3 * X, qx)
-    quantise("lw1", T.w1in, "w", 0, 256, qw)
-    quantise("lw2", T.w2in, "w", 256, W, qw)
+    col = [event(3), event(3), event(3)]
+    z = [(event(), event()) for _ in BATCHES]
+    rows = [(event(2), event(2)) for _ in BATCHES]
+    coded = [event() for _ in BATCHES]
+    size = [X * (c1 - c0) for _, c0, c1 in BATCHES]
+    start = [sum(size[:i]) for i in range(len(BATCHES))]
+    order = [int(t[1:]) for t in TENSOR if t[0] == "z"]
 
-    def x_to(view, i, eng):
-        d = part[i]
+    def bank(i, b):
+        at = 512 * (2 * (order.index(i) % 2) + b)
+        return T.pz[:, at:at + size[i]]
+
+    def row(i, b):
+        return T.h[:, 4 * start[i] + b:4 * (start[i] + size[i]):4]
+
+    def mm(out, w0, xname, x0, n, ev, first=True, last=True):
+        inc(g.tensor.matmul_mx(out, T["qw"][:, w0:w0 + 128], T["pw"][:, w0:w0 + 128],
+                               T["q" + xname][:, x0:x0 + n], T["p" + xname][:, x0:x0 + n], first, last), ev)
+
+    def landed(name):
+        if name[0] == "w":
+            return (name, landing(name))
+        d = part[int(name[1])]
+        return (name, landing("x%d" % partners(d).index(core)) if topo.may_write(d, core) else 2 * nE)
+
+    terms = [0, 0, 0]
+    for t in TENSOR:
+        i = int(t[1:])
+        w, c0, c1 = BATCHES[i]
+        if t[0] == "z":
+            need("T", qx, qw)
+            if w:
+                need("T", landed("w%d" % w))
+            need("T", *[landed("x%d" % c) for c in range(c0, c1) if c < 2])
+            j = order.index(i)
+            if j >= 2:
+                need("T", *rows[order[j - 2]])
+            for b in (0, 1):
+                mm(bank(i, b), W * w + 128 * b, "x", X * c0, size[i], z[i][b])
+        else:
+            need("T", coded[i])
+            for c in range(c0, c1):
+                terms[c] += 1
+                mm(T.po[:, 512 * c:512 * c + 128], W * w + 256, "h", start[i] + X * (c - c0), X, col[c],
+                   terms[c] == 1, terms[c] == 3)
+
+    out = [event(), event()]
+    for t in SCALAR:
+        i = int(t[1:])
+        if t[0] == "a":
+            need("S", z[i][0])
+            for b in (0, 1):
+                inc(g.scalar.activation(row(i, b), bank(i, 0), ActivationFunctionType.Relu, scale=-C if b else C), rows[i][0])
+        else:
+            need("S", col[i])
+            inc(g.scalar.activation(slot("so", i), T.po[:, 512 * i:512 * i + 128], ActivationFunctionType.Copy), out[i])
+
+    for t in VECTOR:
+        i = int(t[1:])
+        if t[0] == "t":
+            need("V", z[i][1])
+            for b in (0, 1):
+                inc(g.vector.tensor_scalar(row(i, 2 + b), bank(i, 1), -C if b else C, 0.0, AluOpType.mult, AluOpType.max),
+                    rows[i][1])
+        else:
+            need("V", *rows[i])
+            a, b = start[i], start[i] + size[i]
+            inc(g.vector.quantize_mx(T.qh[:, a:b], T.ph[:, a:b], T.h[:, 4 * a:4 * b]), coded[i])
+
+    for c in (0, 1):
+        need("g", out[c])
+        d = part[c]
         if topo.may_write(core, d):
             s = partners(d).index(core)
-            return (eng, "x%d" % s, view("x", 2 * X, 3 * X), d, view("x", X * s, X * s + X))
-        return (eng, "rc" if view is codes else "rp", view("x", 2 * X, 3 * X), relays(k)[core], view("x", 0, X))
-
-    need("g", qx)
-    for view in (codes, scales):
-        send(x_to(view, 0, E1), x_to(view, 1, E0))
-    need("g", qw)
-    for i, d in ((1, p1), (2, p2)):
-        for view in (codes, scales):
-            send((allE, "w%d" % i, view("w", 0, W), d, view("w", W * i, W * i + W)))
-
-    last_r = {}
-    col = [event(), event(), event()]
-    st = {"off": 0, "zs": 0, "pend": None, "terms": [0, 0, 0]}
-
-    def mm(out, w0, xname, x0, n, ev, start=True, stop=True):
-        inc(g.tensor.matmul_mx(out, T["qw"][:, w0:w0 + 128], T["pw"][:, w0:w0 + 128],
-                               T["q" + xname][:, x0:x0 + n], T["p" + xname][:, x0:x0 + n], start, stop), ev)
-
-    def finish():
-        if st["pend"] is None:
-            return
-        w, c0, c1, off, q = st["pend"]
-        st["pend"] = None
-        need("T", q)
-        for c in range(c0, c1):
-            n = st["terms"][c]
-            st["terms"][c] += 1
-            mm(T.po[:, 512 * c:512 * c + 128], W * w + 256, "h", off + 128 * (c - c0), 128, col[c], n == 0, n == 2)
-            if n == 2 and c < 2:
-                need("S", col[c])
-                out = event()
-                inc(g.scalar.activation(slot("so", c), T.po[:, 512 * c:512 * c + 128], ActivationFunctionType.Copy), out)
-                need("g", out)
-                d = part[c]
-                if topo.may_write(core, d):
-                    s = partners(d).index(core)
-                    send((allE, "s%d" % s, slot("so", c), d, slot("si", s)))
-                else:
-                    send((allE, "rs", slot("so", c), relays(k)[core], slot("si", 0)))
-
-    def batch(arrived, w, c0, c1, alone=False, hurry=False):
-        if alone:
-            finish()
-        n = X * (c1 - c0)
-        off, zs = st["off"], st["zs"]
-        st["off"], st["zs"] = off + n, 1 - zs
-        z, r, q = [event(), event()], [event(), event()], event()
-        need("T", *arrived)
-        need("T", *last_r.get(zs, []))
-        last_r[zs] = r
-
-        def bank(b):
-            return T.pz[:, 512 * (2 * zs + b):512 * (2 * zs + b) + n]
-
-        def rows(b):
-            return T.h[:, 4 * off + b:4 * (off + n):4]
-
-        for b in (0, 1):
-            mm(bank(b), W * w + 128 * b, "x", X * c0, n, z[b])
-        if hurry:
-            finish()
-        need("S", z[0])
-        for b in (0, 1):
-            inc(g.scalar.activation(rows(b), bank(0), ActivationFunctionType.Relu, scale=-C if b else C), r[0])
-        need("V", z[1])
-        for b in (0, 1):
-            inc(g.vector.tensor_scalar(rows(2 + b), bank(1), -C if b else C, 0.0, AluOpType.mult, AluOpType.max), r[1])
-        need("V", *r)
-        inc(g.vector.quantize_mx(T.qh[:, off:off + n], T.ph[:, off:off + n], T.h[:, 4 * off:4 * (off + n)]), q)
-        finish()
-        st["pend"] = (w, c0, c1, off, q)
-
-    x_in = [["x%d" % i, 2 * (hE if topo.may_write(core, part[i]) else nE)] for i in (0, 1)]
-    w_in = [None, ["w1", 2 * nE], ["w2", 2 * nE]]
-    batch([qx, qw], 0, 2, 3)
-    batch([x_in[1]], 0, 1, 2, alone=True)
-    batch([w_in[1]], 1, 1, 3, alone=True)
-    batch([x_in[0]], 0, 0, 1, alone=True)
-    batch([], 1, 0, 1)
-    batch([w_in[2]], 2, 0, 1, alone=True)
-    batch([], 2, 1, 2, hurry=True)
-    batch([], 2, 2, 3, hurry=True)
-    finish()
+            send(("off", "s%d" % s, slot("so", c), d, slot("si", s)))
+        else:
+            send(("off", "rs", slot("so", c), relays(k)[core], slot("si", 0)))
 
     first, fin = event(), event()
-    need("V", col[2], ["s1", nE])
+    need("V", col[2], ("s1", nE))
     inc(g.vector.tensor_tensor(slot("acc", 0), T.po[:, 1024:1152], slot("si", 1), AluOpType.add), first)
-    need("V", first, ["s0", nE])
+    need("V", first, ("s0", nE))
     inc(g.vector.tensor_tensor(slot("acc", 1), slot("acc", 0), slot("si", 0), AluOpType.add), fin)
     need("Y", fin)
     g.sync.dma_start(T.y[:], slot("acc", 1)).then_inc(T.sem["stored"], 16)

import numpy as np
from concourse.bass import DstId, RemoteDMATransfer
from concourse.mybir import dt, AluOpType, ActivationFunctionType

C = float(np.float32(0.047))
WORLD = 512
X, W = 128, 384
F8, U8, BF, F32 = "float8_e4m3fn_x4", "uint8", "bfloat16", "float32"

SENDS = [("x", "c", [[("x0", "off"), ("h", "on")]]),
         ("x", "p", [[("x0", "off"), ("h", "on")]]),
         ("w", "c", [[("w1", "off"), ("h", "on")]]),
         ("w", "p", [[("w1", "off")], [("w2", "off")]])]
HELPER = [("x", "c", [[("x1", "off")]]),
          ("x", "p", [[("x1", "off")]]),
          ("w", "c", [[("w2", "off")]])]

BATCHES = [(0, 2, 3), (0, 1, 2), (1, 1, 3), (0, 0, 1), (1, 0, 1), (2, 0, 1), (2, 1, 3)]
TENSOR = "z0 o0 z1 z2 z3 o1 z4 z5 o2 o3 z6 o4 o5 o6".split()
SCALAR = "a0 a1 a2 a3 a4 a5 a6 c0 c1".split()
VECTOR = "t0 q0 t1 q1 t2 t3 q2 q3 t4 t5 q4 q5 t6 q6".split()

SCRATCH = {
    "xin": ("sbuf", [128, 512], BF), "w1in": ("sbuf", [128, 1024], BF), "w2in": ("sbuf", [128, 512], BF),
    "h": ("sbuf", [128, 4 * 1152], BF),
    "so": ("sbuf", [128, 2 * 128], F32),
    "si": ("sbuf", [128, 2 * 128], F32),
    "acc": ("sbuf", [128, 2 * 128], F32),
    "pz": ("psum", [128, 2048], F32),
    "po": ("psum", [128, 1536], F32),
}
for _n, _w in (("x", 3 * X),
               ("w", 3 * W),
               ("h", 1152)):
    SCRATCH["q" + _n] = ("sbuf", [128, _w], F8)
    SCRATCH["p" + _n] = ("sbuf", [128, _w], U8)

EVENTS = 60
SEMAPHORES = (["lx", "lw1", "lw2", "sent", "stored",
               "x0", "x1", "w1", "w2", "s0", "s1",
               "xc", "xp", "wc", "wp", "rs"]
              + ["e%d" % i for i in range(EVENTS)])


def rank_program(g, core, T, topo):
    hosts = sorted({topo.host(c) for c in T.cores})
    group = {h: sorted((c for c in T.cores if topo.host(c) == h), key=topo.chip) for h in hosts}
    mid = [h for h in hosts if all(topo.may_write(a, b) for a in group[h] for b in T.cores if b != a)][0]
    near, far = sorted((h for h in hosts if h != mid), key=lambda h: not topo.same_plane(group[h][0], group[mid][0]))

    def helper(c):
        return [e for e in range(WORLD) if topo.host(e) == topo.host(c) and topo.chip(e) == topo.chip(c)
                and topo.die(e) != topo.die(c)][0]

    def partners(c):
        k = group[topo.host(c)].index(c)
        return [group[h][k] for h in {mid: (far, near), near: (far, mid), far: (near, mid)}[topo.host(c)]]

    def relays(k):
        a, b = group[near][k], group[far][k]
        out = [c for c in range(WORLD) if topo.host(c) not in hosts and topo.chip(c) == topo.chip(a)
               and topo.die(c) == topo.die(a)
               and all(topo.may_write(c, d) and topo.may_write(d, c) for d in (a, b))]
        return {a: out[0], b: out[1]}

    def bits(m):
        return [e for e in range(m.bit_length()) if (m >> e) & 1]

    a, b = group[mid][:2]
    ENG = {"off": bits(topo.mask(a, b))}
    ENG["on"] = [e for e in bits(topo.mask(a, helper(a))) if e not in ENG["off"]]
    nE = len(ENG["off"])
    sent = ["sent", 0]

    def send(*transfers):
        out = []
        for eng, sem, src, d, dst in transfers:
            rid, pid = topo.addr(d, core)
            out.append(RemoteDMATransfer(dst_ids=[DstId(rid=rid, pnc=pid)], dma_engine_mask=sum(1 << e for e in ENG[eng]),
                                         remote_sem=T.sem[sem], srcs=[src], dsts=[dst]))
            sent[1] += len(ENG[eng])
        g.remote_dma_fused(out, local_sem=T.sem["sent"])

    def codes(name, a, b):
        return T["q" + name][:, a:b].bitcast(dt.uint8)

    def scales(name, a, b):
        return T["p" + name][:, a:b]

    VIEW = {"c": codes, "p": scales}
    WIDTH = {"x": X, "w": W}

    def slot(buf, i):
        return T[buf][:, 128 * i:128 * (i + 1)]

    def landing(target, v=None):
        return sum(len(ENG[e]) for _, w, calls in SENDS + HELPER if v in (None, w) for call in calls for t, e in call if t == target)

    def goes(owner, what, v, target, eng, src):
        view, k = VIEW[v], group[topo.host(owner)].index(owner)
        if target == "h":
            return (eng, what + v, src, helper(owner), view(what, 0, WIDTH[what]))
        i = int(target[1])
        if what == "w":
            return (eng, target, src, group[topo.host(owner)][(k + i) % 3], view("w", W * i, W * i + W))
        d = partners(owner)[i]
        if topo.may_write(owner, d):
            s = partners(d).index(owner)
            return (eng, "x%d" % s, src, d, view("x", X * s, X * s + X))
        return (eng, "x" + v, src, relays(k)[owner], view("x", 0, X))

    if T.rank_of(core) is None:
        for k in range(len(group[near])):
            r = relays(k)
            for src, dst in ((group[near][k], group[far][k]), (group[far][k], group[near][k])):
                if r[src] == core:
                    s = partners(dst).index(src)
                    for v in "cp":
                        g.wait_ge(T.sem["x" + v], landing("x0", v))
                        send(("off", "x%d" % s, VIEW[v]("x", 0, X), dst, VIEW[v]("x", X * s, X * s + X)))
                    g.wait_ge(T.sem["rs"], nE)
                    send(("off", "s%d" % s, slot("si", 0), dst, slot("si", s)))
                    g.wait_ge(T.sem["sent"], sent[1])
        for owner in T.cores:
            if helper(owner) == core:
                for what, v, calls in HELPER:
                    g.wait_ge(T.sem[what + v], sum(len(ENG[e]) for k, w, cs in SENDS if (k, w) == (what, v)
                                                   for call in cs for t, e in call if t == "h"))
                    for call in calls:
                        send(*[goes(owner, what, v, t, e, VIEW[v](what, 0, WIDTH[what])) for t, e in call])
                g.wait_ge(T.sem["sent"], sent[1])
        return

    me = topo.host(core)
    k = group[me].index(core)
    part = partners(core)

    ev_n = [0]

    def event(n=1):
        ev_n[0] += 1
        return ("e%d" % (ev_n[0] - 1), n)

    def inc(call, ev):
        call.then_inc(T.sem[ev[0]], 1)

    queues = {"g": g, "T": g.tensor, "V": g.vector, "S": g.scalar, "Y": g.sync}
    waited = {q: set() for q in queues}

    def need(q, *evs):
        for ev in evs:
            if ev[0] not in waited[q]:
                queues[q].wait_ge(T.sem[ev[0]], ev[1])
                waited[q].add(ev[0])

    for name in ("x", "w1", "w2"):
        g.sync.dma_start(T[name + "in"][:], T[name][:]).then_inc(T.sem["l" + name], 16)
    qx, qw = event(), event(2)
    for name, to, c0, c1, ev in (("x", "x", 2 * X, 3 * X, qx), ("w1", "w", 0, 256, qw), ("w2", "w", 256, W, qw)):
        need("V", ("l" + name, 16))
        inc(g.vector.quantize_mx(T["q" + to][:, c0:c1], T["p" + to][:, c0:c1], T[name + "in"][:]), ev)

    for what, v, calls in SENDS:
        need("g", qx if what == "x" else qw)
        src = VIEW[v]("x", 2 * X, 3 * X) if what == "x" else VIEW[v]("w", 0, W)
        for call in calls:
            send(*[goes(core, what, v, t, e, src) for t, e in call])

    col = [event(3), event(3), event(3)]
    z = [(event(), event()) for _ in BATCHES]
    rows = [(event(2), event(2)) for _ in BATCHES]
    coded = [event() for _ in BATCHES]
    size = [X * (c1 - c0) for _, c0, c1 in BATCHES]
    start = [sum(size[:i]) for i in range(len(BATCHES))]
    order = [int(t[1:]) for t in TENSOR if t[0] == "z"]

    def bank(i, b):
        at = 512 * (2 * (order.index(i) % 2) + b)
        return T.pz[:, at:at + size[i]]

    def row(i, b):
        return T.h[:, 4 * start[i] + b:4 * (start[i] + size[i]):4]

    def mm(out, w0, xname, x0, n, ev, first=True, last=True):
        inc(g.tensor.matmul_mx(out, T["qw"][:, w0:w0 + 128], T["pw"][:, w0:w0 + 128],
                               T["q" + xname][:, x0:x0 + n], T["p" + xname][:, x0:x0 + n], first, last), ev)

    def landed(name):
        if name[0] == "w":
            return (name, landing(name))
        d = part[int(name[1])]
        return (name, landing("x%d" % partners(d).index(core)) if topo.may_write(d, core) else 2 * nE)

    terms = [0, 0, 0]
    for t in TENSOR:
        i = int(t[1:])
        w, c0, c1 = BATCHES[i]
        if t[0] == "z":
            need("T", qx, qw)
            if w:
                need("T", landed("w%d" % w))
            need("T", *[landed("x%d" % c) for c in range(c0, c1) if c < 2])
            j = order.index(i)
            if j >= 2:
                need("T", *rows[order[j - 2]])
            for b in (0, 1):
                mm(bank(i, b), W * w + 128 * b, "x", X * c0, size[i], z[i][b])
        else:
            need("T", coded[i])
            for c in range(c0, c1):
                terms[c] += 1
                mm(T.po[:, 512 * c:512 * c + 128], W * w + 256, "h", start[i] + X * (c - c0), X, col[c],
                   terms[c] == 1, terms[c] == 3)

    out = [event(), event()]
    for t in SCALAR:
        i = int(t[1:])
        if t[0] == "a":
            need("S", z[i][0])
            for b in (0, 1):
                inc(g.scalar.activation(row(i, b), bank(i, 0), ActivationFunctionType.Relu, scale=-C if b else C), rows[i][0])
        else:
            need("S", col[i])
            inc(g.scalar.activation(slot("so", i), T.po[:, 512 * i:512 * i + 128], ActivationFunctionType.Copy), out[i])

    for t in VECTOR:
        i = int(t[1:])
        if t[0] == "t":
            need("V", z[i][1])
            for b in (0, 1):
                inc(g.vector.tensor_scalar(row(i, 2 + b), bank(i, 1), -C if b else C, 0.0, AluOpType.mult, AluOpType.max),
                    rows[i][1])
        else:
            need("V", *rows[i])
            a, b = start[i], start[i] + size[i]
            inc(g.vector.quantize_mx(T.qh[:, a:b], T.ph[:, a:b], T.h[:, 4 * a:4 * b]), coded[i])

    for c in (0, 1):
        need("g", out[c])
        d = part[c]
        if topo.may_write(core, d):
            s = partners(d).index(core)
            send(("off", "s%d" % s, slot("so", c), d, slot("si", s)))
        else:
            send(("off", "rs", slot("so", c), relays(k)[core], slot("si", 0)))

    first, fin = event(), event()
    need("V", col[2], ("s1", nE))
    inc(g.vector.tensor_tensor(slot("acc", 0), T.po[:, 1024:1152], slot("si", 1), AluOpType.add), first)
    need("V", first, ("s0", nE))
    inc(g.vector.tensor_tensor(slot("acc", 1), slot("acc", 0), slot("si", 0), AluOpType.add), fin)
    need("Y", fin)
    g.sync.dma_start(T.y[:], slot("acc", 1)).then_inc(T.sem["stored"], 16)
    g.sync.wait_ge(T.sem["stored"], 16)
    need("g", sent)
